import numpy as np
import ml_dtypes

BF16 = ml_dtypes.bfloat16


def bf(x):
    return np.asarray(x, np.float32).astype(BF16)


def f32(x):
    return np.asarray(x, np.float32)


def f64(x):
    return np.asarray(x).astype(np.float64)


def striped(idx):
    return np.tile(idx.reshape(-1, 16).T, (8, 1))


S, K, M, N, E, Q = 512, 512, 128, 512, 4, 128


def gelu_tanh(v):
    return 0.5 * v * (1.0 + np.tanh(np.sqrt(2.0 / np.pi) * (v + 0.044715 * v**3)))


def setup_inputs():
    return {"base": bf(np.random.standard_normal((M, S))), "x": bf(np.random.standard_normal((K, N))), "w": bf(np.random.standard_normal((E, K, M)) / np.sqrt(K)), "b": f32(0.5 * np.random.standard_normal((M, 1))), "offs": striped(np.random.permutation(S))}


def reference(base, x, w, b, offs):
    idx = offs[:16].T.reshape(-1)
    z = f64(base).copy()
    for e in range(E):
        z[:, idx[e * Q : (e + 1) * Q]] += f64(w)[e].T @ f64(x)[:, e * Q : (e + 1) * Q]
    return gelu_tanh(z + f64(b))

@@ -1,0 +1,59 @@
+import concourse.mybir as mybir
+from concourse.masks import make_identity
+
+P = 128
+S = 512
+K = 512
+E = 4
+Q = 128
+KB = K // P
+QC = Q // 16
+
+FLOPS = 2 * K * P * E * Q
+
+BF16 = mybir.dt.bfloat16
+F32 = mybir.dt.float32
+U16 = mybir.dt.uint16
+
+
+def tile_scatter_matmul_kernel(tc, base, x, w, b, offs, out):
+    nc = tc.nc
+    with (
+        tc.tile_pool(name="held", bufs=1) as held,
+        tc.psum_pool(name="psum", bufs=1) as psum,
+    ):
+        offsets = held.tile([P, E * QC], U16, name="offsets")
+        nc.sync.dma_start(offsets[:], offs)
+        base_sb = held.tile([P, S], BF16, name="base_sb")
+        nc.scalar.dma_start(base_sb[:], base)
+        x_sb = held.tile([P, KB, E * Q], BF16, name="x_sb")
+        nc.sync.dma_start(x_sb[:], x.rearrange("(kb p) j -> p kb j", p=P))
+        w_sb = held.tile([P, E * KB, P], BF16, name="w_sb")
+        nc.scalar.dma_start(w_sb[:], w.rearrange("e (kb p) m -> p (e kb) m", p=P))
+        bias = held.tile([P, 1], F32, name="bias")
+        nc.gpsimd.dma_start(bias[:], b)
+
+        ident = held.tile([P, P], BF16, name="ident")
+        make_identity(nc, ident[:])
+
+        window = psum.tile([P, S], F32, name="window")
+        nc.tensor.matmul(window[:], ident[:], base_sb[:], start=True, stop=False)
+
+        for e in range(E):
+            for kb in range(KB):
+                nc.tensor.matmul(
+                    window[:].indirect(offsets[:, e * QC : (e + 1) * QC]),
+                    w_sb[:, e * KB + kb, :],
+                    x_sb[:, kb, e * Q : (e + 1) * Q],
+                    start=False,
+                    stop=(e == E - 1 and kb == KB - 1),
+                )
+
+        result = held.tile([P, S], F32, name="result")
+        nc.scalar.activation(
+            result[:],
+            window[:],
+            mybir.ActivationFunctionType.Gelu_apprx_tanh,
+            bias=bias[:],
+        )
+        nc.sync.dma_start(out, result[:])

@@ -8,6 +8,7 @@ E = 4
 Q = 128
 KB = K // P
 QC = Q // 16
+WARM = 3
 
 FLOPS = 2 * K * P * E * Q
 
@@ -23,30 +24,42 @@ def tile_scatter_matmul_kernel(tc, base, x, w, b, offs, out):
         tc.psum_pool(name="psum", bufs=1) as psum,
     ):
         offsets = held.tile([P, E * QC], U16, name="offsets")
-        nc.sync.dma_start(offsets[:], offs)
-        base_sb = held.tile([P, S], BF16, name="base_sb")
-        nc.scalar.dma_start(base_sb[:], base)
-        x_sb = held.tile([P, KB, E * Q], BF16, name="x_sb")
-        nc.sync.dma_start(x_sb[:], x.rearrange("(kb p) j -> p kb j", p=P))
-        w_sb = held.tile([P, E * KB, P], BF16, name="w_sb")
-        nc.scalar.dma_start(w_sb[:], w.rearrange("e (kb p) m -> p (e kb) m", p=P))
         bias = held.tile([P, 1], F32, name="bias")
-        nc.gpsimd.dma_start(bias[:], b)
+        base_sb = held.tile([P, S], BF16, name="base_sb")
+        x_sb = [held.tile([P, E * Q], BF16, name=f"x_sb{kb}") for kb in range(KB)]
+        w_sb = [held.tile([P, KB, P], BF16, name=f"w_sb{e}") for e in range(E)]
+
+        x_view = x.rearrange("(p kb) j -> p kb j", kb=KB)
+        loads = [(base_sb, base), (x_sb[0], x_view[:, 0, :])]
+        loads += [(w_sb[e], w[e].rearrange("(p kb) m -> p kb m", kb=KB)) for e in range(E)]
+        loads += [(x_sb[kb], x_view[:, kb, :]) for kb in range(1, KB)]
+
+        nc.sync.dma_start(offsets[:], offs)
+        nc.scalar.dma_start(bias[:], b)
+        queues = [nc.sync, nc.scalar]
+        for i, (tile, source) in enumerate(loads):
+            queues[i % 2].dma_start(tile[:], source)
 
         ident = held.tile([P, P], BF16, name="ident")
         make_identity(nc, ident[:])
 
+        zeros = held.tile([P, S], BF16, name="zeros")
+        nc.vector.memset(zeros[:], 0.0)
+        warm_ps = psum.tile([P, S], F32, name="warm_ps")
+        for i in range(WARM):
+            nc.tensor.matmul(warm_ps[:], ident[:], zeros[:], start=True, stop=True)
+
         window = psum.tile([P, S], F32, name="window")
         nc.tensor.matmul(window[:], ident[:], base_sb[:], start=True, stop=False)
 
-        for e in range(E):
-            for kb in range(KB):
+        for kb in range(KB):
+            for e in range(E):
                 nc.tensor.matmul(
                     window[:].indirect(offsets[:, e * QC : (e + 1) * QC]),
-                    w_sb[:, e * KB + kb, :],
-                    x_sb[:, kb, e * Q : (e + 1) * Q],
+                    w_sb[e][:, kb, :],
+                    x_sb[kb][:, e * Q : (e + 1) * Q],
                     start=False,
-                    stop=(e == E - 1 and kb == KB - 1),
+                    stop=(kb == KB - 1 and e == E - 1),
                 )
 
         result = held.tile([P, S], F32, name="result")

@@ -9,6 +9,8 @@ Q = 128
 KB = K // P
 QC = Q // 16
 WARM = 3
+H = 2
+SH = S // H
 
 FLOPS = 2 * K * P * E * Q
 
@@ -62,11 +64,12 @@ def tile_scatter_matmul_kernel(tc, base, x, w, b, offs, out):
                     stop=(kb == KB - 1 and e == E - 1),
                 )
 
-        result = held.tile([P, S], F32, name="result")
-        nc.scalar.activation(
-            result[:],
-            window[:],
-            mybir.ActivationFunctionType.Gelu_apprx_tanh,
-            bias=bias[:],
-        )
-        nc.sync.dma_start(out, result[:])
+        for h in range(H):
+            result = held.tile([P, SH], F32, name=f"result{h}")
+            nc.scalar.activation(
+                result[:],
+                window[:, h * SH : (h + 1) * SH],
+                mybir.ActivationFunctionType.Gelu_apprx_tanh,
+                bias=bias[:],
+            )
+            nc.sync.dma_start(out[:, h * SH : (h + 1) * SH], result[:])

@@ -32,15 +32,13 @@ def tile_scatter_matmul_kernel(tc, base, x, w, b, offs, out):
         w_sb = [held.tile([P, KB, P], BF16, name=f"w_sb{e}") for e in range(E)]
 
         x_view = x.rearrange("(p kb) j -> p kb j", kb=KB)
-        loads = [(base_sb, base), (x_sb[0], x_view[:, 0, :])]
-        loads += [(w_sb[e], w[e].rearrange("(p kb) m -> p kb m", kb=KB)) for e in range(E)]
-        loads += [(x_sb[kb], x_view[:, kb, :]) for kb in range(1, KB)]
 
         nc.sync.dma_start(offsets[:], offs)
         nc.scalar.dma_start(bias[:], b)
-        queues = [nc.sync, nc.scalar]
-        for i, (tile, source) in enumerate(loads):
-            queues[i % 2].dma_start(tile[:], source)
+        nc.sync.dma_start(base_sb[:], base)
+        for s in range(E):
+            nc.scalar.dma_start(x_sb[s][:], x_view[:, s, :])
+            nc.sync.dma_start(w_sb[s][:], w[s].rearrange("(p kb) m -> p kb m", kb=KB))
 
         ident = held.tile([P, P], BF16, name="ident")
         make_identity(nc, ident[:])
@@ -54,15 +52,18 @@ def tile_scatter_matmul_kernel(tc, base, x, w, b, offs, out):
         window = psum.tile([P, S], F32, name="window")
         nc.tensor.matmul(window[:], ident[:], base_sb[:], start=True, stop=False)
 
-        for kb in range(KB):
-            for e in range(E):
-                nc.tensor.matmul(
-                    window[:].indirect(offsets[:, e * QC : (e + 1) * QC]),
-                    w_sb[e][:, kb, :],
-                    x_sb[kb][:, e * Q : (e + 1) * Q],
-                    start=False,
-                    stop=(kb == KB - 1 and e == E - 1),
-                )
+        order = []
+        for s in range(E):
+            order += [(s, e) for e in range(s)]
+            order += [(kb, s) for kb in range(s + 1)]
+        for kb, e in order:
+            nc.tensor.matmul(
+                window[:].indirect(offsets[:, e * QC : (e + 1) * QC]),
+                w_sb[e][:, kb, :],
+                x_sb[kb][:, e * Q : (e + 1) * Q],
+                start=False,
+                stop=((kb, e) == order[-1]),
+            )
 
         for h in range(H):
             result = held.tile([P, SH], F32, name=f"result{h}")

@@ -8,7 +8,7 @@ E = 4
 Q = 128
 KB = K // P
 QC = Q // 16
-WARM = 3
+WARM = 10
 H = 2
 SH = S // H
 
@@ -40,14 +40,14 @@ def tile_scatter_matmul_kernel(tc, base, x, w, b, offs, out):
             nc.scalar.dma_start(x_sb[s][:], x_view[:, s, :])
             nc.sync.dma_start(w_sb[s][:], w[s].rearrange("(p kb) m -> p kb m", kb=KB))
 
+        zeros = held.tile([P, P], BF16, name="zeros")
+        nc.vector.memset(zeros[:], 0.0)
+        warm_ps = psum.tile([P, P], F32, name="warm_ps")
+        for i in range(WARM):
+            nc.tensor.matmul(warm_ps[:], zeros[:], zeros[:], start=True, stop=True)
+
         ident = held.tile([P, P], BF16, name="ident")
         make_identity(nc, ident[:])
-
-        zeros = held.tile([P, S], BF16, name="zeros")
-        nc.vector.memset(zeros[:], 0.0)
-        warm_ps = psum.tile([P, S], F32, name="warm_ps")
-        for i in range(WARM):
-            nc.tensor.matmul(warm_ps[:], ident[:], zeros[:], start=True, stop=True)
 
         window = psum.tile([P, S], F32, name="window")
         nc.tensor.matmul(window[:], ident[:], base_sb[:], start=True, stop=False)

import concourse.mybir as mybir
from concourse.masks import make_identity

P = 128
S = 512
K = 512
E = 4
Q = 128
KB = K // P
QC = Q // 16
WARM = 10
H = 2
SH = S // H

FLOPS = 2 * K * P * E * Q

BF16 = mybir.dt.bfloat16
F32 = mybir.dt.float32
U16 = mybir.dt.uint16


def tile_scatter_matmul_kernel(tc, base, x, w, b, offs, out):
    nc = tc.nc
    with (
        tc.tile_pool(name="held", bufs=1) as held,
        tc.psum_pool(name="psum", bufs=1) as psum,
    ):
        offsets = held.tile([P, E * QC], U16, name="offsets")
        bias = held.tile([P, 1], F32, name="bias")
        base_sb = held.tile([P, S], BF16, name="base_sb")
        x_sb = [held.tile([P, E * Q], BF16, name=f"x_sb{kb}") for kb in range(KB)]
        w_sb = [held.tile([P, KB, P], BF16, name=f"w_sb{e}") for e in range(E)]

        x_view = x.rearrange("(p kb) j -> p kb j", kb=KB)

        nc.sync.dma_start(offsets[:], offs)
        nc.scalar.dma_start(bias[:], b)
        nc.sync.dma_start(base_sb[:], base)
        for s in range(E):
            nc.scalar.dma_start(x_sb[s][:], x_view[:, s, :])
            nc.sync.dma_start(w_sb[s][:], w[s].rearrange("(p kb) m -> p kb m", kb=KB))

        zeros = held.tile([P, P], BF16, name="zeros")
        nc.vector.memset(zeros[:], 0.0)
        warm_ps = psum.tile([P, P], F32, name="warm_ps")
        for i in range(WARM):
            nc.tensor.matmul(warm_ps[:], zeros[:], zeros[:], start=True, stop=True)

        ident = held.tile([P, P], BF16, name="ident")
        make_identity(nc, ident[:])

        window = psum.tile([P, S], F32, name="window")
        nc.tensor.matmul(window[:], ident[:], base_sb[:], start=True, stop=False)

        order = []
        for s in range(E):
            order += [(s, e) for e in range(s)]
            order += [(kb, s) for kb in range(s + 1)]
        for kb, e in order:
            nc.tensor.matmul(
                window[:].indirect(offsets[:, e * QC : (e + 1) * QC]),
                w_sb[e][:, kb, :],
                x_sb[kb][:, e * Q : (e + 1) * Q],
                start=False,
                stop=((kb, e) == order[-1]),
            )

        for h in range(H):
            result = held.tile([P, SH], F32, name=f"result{h}")
            nc.scalar.activation(
                result[:],
                window[:, h * SH : (h + 1) * SH],
                mybir.ActivationFunctionType.Gelu_apprx_tanh,
                bias=bias[:],
            )
            nc.sync.dma_start(out[:, h * SH : (h + 1) * SH], result[:])
